import numpy as np
import ml_dtypes


def mxq(x, axis, fmt="e4m3"):
    dtype, down = {"e4m3": (ml_dtypes.float8_e4m3fn, 7), "e5m2": (ml_dtypes.float8_e5m2, 14)}[fmt]
    v = np.moveaxis(np.asarray(x, np.float32).astype(ml_dtypes.bfloat16).astype(np.float64), axis, -1)
    blocks = v.reshape(v.shape[:-1] + (-1, 32))
    amax = np.abs(blocks).max(-1, keepdims=True)
    byte = np.maximum(np.where(amax > 0, np.frexp(amax)[1] - 1 + 127, 0) - down, 1)
    scale = np.exp2(byte - 127.0)
    codes = (blocks / scale).astype(np.float32).astype(dtype).astype(np.float64)
    return np.moveaxis((codes * scale).reshape(v.shape), -1, axis)


WIDE = False


def mx_kscale(k):
    if not WIDE:
        return np.ones(k)
    levels = np.array([10, -10, 5, -5, 0])
    if k % 512:
        return np.exp2(np.random.permutation(np.resize(levels, k // 32))).repeat(32)
    a = np.empty((k // 512, 16))
    for p in range(k // 512):
        a[p, :8] = np.random.permutation(np.resize(levels, 8))
        for g in range(8):
            far = levels[np.abs(levels - a[p, g]) >= 10]
            a[p, g + 8] = far[np.random.randint(len(far))]
    return np.exp2(a.ravel()).repeat(32)


def f64(x):
    return np.asarray(x).astype(np.float64)


def striped8(idx):
    return np.concatenate([x.reshape(-1, 16).T for x in idx]).astype(np.uint16)


def runs(offs, k):
    lists = np.stack([offs[16 * r : 16 * r + 16].T.reshape(-1) for r in range(8)]).astype(np.int64)
    return lists[np.arange(k) % 512 // 64]


def pack_weight(w):
    k, n = w.shape
    w = f64(np.asarray(w, np.float32).astype(ml_dtypes.bfloat16)).reshape(k // 32, 32, n)
    amax = np.abs(w).max(1)
    byte = np.clip(np.where(amax > 0, np.frexp(amax)[1] - 1 + 127 - 7, 1), 1, 254)
    scaled = (w * np.exp2(127.0 - byte)[:, None, :]).reshape(k, n).astype(np.float32)
    words = np.ascontiguousarray(scaled.reshape(k // 512, 128, 4, n).transpose(0, 1, 3, 2)).astype(ml_dtypes.float8_e4m3fn).view(np.uint8)
    return words, np.ascontiguousarray(byte.astype(np.uint8).reshape(k // 512, 16, n))


def unpack_weight(words, scales):
    g, p, n, _ = words.shape
    vals = np.ascontiguousarray(words).view(ml_dtypes.float8_e4m3fn).astype(np.float64) * np.repeat(np.exp2(scales.astype(np.float64) - 127.0), 8, axis=1)[..., None]
    return vals.transpose(0, 1, 3, 2).reshape(g * 512, n)


def silu(v):
    return v / (1.0 + np.exp(-np.maximum(v, -700.0)))


K, T, S, N = 1024, 2048, 512, 128


def setup_inputs():
    n = np.random.standard_normal
    s = mx_kscale(K)[:, None]
    packed_xT = pack_weight(n((K, T)) * s)
    return {
        "x_words": packed_xT[0],
        "x_scales": packed_xT[1],
        "w1": (n((K, N)) / np.sqrt(K) / s).astype(np.float32),
        "w2": (n((K, N)) / np.sqrt(K) / s).astype(np.float32),
        "offs": striped8(np.stack([np.random.permutation(T)[:S] for _ in range(8)])),
    }


def reference(x_words, x_scales, w1, w2, offs):
    xq = unpack_weight(x_words, x_scales)[np.arange(K)[:, None], runs(offs, K)]
    return (silu(mxq(f64(w1), 0, "e4m3").T @ xq)) * ((mxq(f64(w2), 0, "e4m3").T @ xq))

@@ -1,0 +1,133 @@
+from contextlib import ExitStack
+
+import concourse.mybir as mybir
+
+K, T, S, N = 1024, 2048, 512, 128
+FLOPS = 2 * 2 * K * S * N
+
+F32 = mybir.dt.float32
+BF16 = mybir.dt.bfloat16
+I32 = mybir.dt.int32
+U32 = mybir.dt.uint32
+U16 = mybir.dt.uint16
+U8 = mybir.dt.uint8
+FP8X4 = mybir.dt.float8_e4m3fn_x4
+SILU = mybir.ActivationFunctionType.Silu
+MULT = mybir.AluOpType.mult
+
+P = 128
+PACK = 4
+K_PASS = P * PACK
+PASSES = K // K_PASS
+HALF = S // 2
+PLANE = 8
+
+
+def tile_picked_phglu_silu_p_kernel(tc, x_words, x_scales, w1, w2, offs, out):
+    nc = tc.nc
+    with ExitStack() as ctx:
+        keep = ctx.enter_context(tc.tile_pool(name="keep", bufs=1))
+        psum = ctx.enter_context(tc.psum_pool(name="psum", bufs=1))
+
+        offsets = keep.tile([P, S // 16], U16, name="offsets")
+        nc.sync.dma_start(offsets[:], offs)
+
+        scale_table = keep.tile([P, T], U8, name="scale_table", align_bytes=64)
+        nc.vector.memset(scale_table[:].bitcast(I32), 0)
+        rows = x_scales.bitcast(I32).rearrange("z (r e) c -> e r z c", e=2)
+        for e in range(2):
+            nc.gpsimd.dma_start(out=scale_table[e:P:PLANE, :].bitcast(I32), in_=rows[e])
+
+        warm = keep.tile([P, 2], F32, name="warm")
+        nc.vector.memset(warm[:, 0:1], 0.0)
+        nc.scalar.activation(warm[:, 1:2], warm[:, 0:1], SILU)
+
+        word_table = [keep.tile([P, T], U32, name="word_table%d" % z, align_bytes=64) for z in range(PASSES)]
+        raw = {}
+
+        def load_words(z):
+            nc.sync.dma_start(out=word_table[z][:].bitcast(I32), in_=x_words[z].rearrange("p n t -> p (n t)").bitcast(I32))
+
+        def load_weight(i, z):
+            raw[i, z] = keep.tile([P, PACK, N], F32, name="raw%d%d" % (i, z), align_bytes=64)
+            w = (w1, w2)[i]
+            nc.sync.dma_start(out=raw[i, z][:], in_=w[z * K_PASS : (z + 1) * K_PASS, :].rearrange("(p j) n -> p j n", j=PACK))
+
+        load_words(0)
+        load_weight(0, 0)
+        load_words(1)
+        load_weight(0, 1)
+        load_weight(1, 0)
+        load_weight(1, 1)
+
+        picked_scales = keep.tile([P, S], U8, name="picked_scales", align_bytes=64)
+        nc.vector.tensor_copy(picked_scales[:], scale_table[:].indirect(offsets[:]))
+        x_planes = keep.tile([P, S], U8, name="x_planes", align_bytes=64)
+        nc.vector.tensor_copy(x_planes[:].bitcast(I32), picked_scales[:].bitcast(I32))
+        for z in range(PASSES):
+            for e in range(2):
+                nc.scalar.dma_start(
+                    out=x_planes[PLANE * z + 2 + e : P : 32, :].bitcast(I32),
+                    in_=picked_scales[16 + PLANE * z + e : P : 32, :].bitcast(I32),
+                )
+
+        picked = [keep.tile([P, S], U32, name="picked%d" % z, align_bytes=64) for z in range(PASSES)]
+        nc.vector.tensor_copy(picked[0][:], word_table[0][:].indirect(offsets[:]))
+
+        codes, planes = {}, {}
+
+        def quantise(i, z, engine):
+            grouped = keep.tile([P, N, PACK], BF16, name="grouped%d%d" % (i, z), align_bytes=64)
+            dst = grouped[:].rearrange("p (c i) j -> p c j i", i=4)
+            src = raw[i, z][:].rearrange("p j (c i) -> p c j i", i=4)
+            if engine == "scalar":
+                nc.scalar.copy(dst, src)
+            else:
+                nc.vector.tensor_copy(dst, src)
+            codes[i, z] = keep.tile([P, N], U32, name="codes%d%d" % (i, z), align_bytes=64)
+            planes[i, z] = keep.tile([P, N], U8, name="planes%d%d" % (i, z), align_bytes=64)
+            nc.vector.quantize_mx(
+                out=codes[i, z][:].bitcast(FP8X4),
+                scales=planes[i, z][:],
+                in_=grouped[:].rearrange("p n j -> p (n j)"),
+            )
+
+        quantise(0, 0, "scalar")
+        for h in range(2):
+            nc.vector.tensor_copy(
+                picked[1][:, h * HALF : (h + 1) * HALF],
+                word_table[1][:].indirect(offsets[:, h * HALF // 16 : (h + 1) * HALF // 16]),
+            )
+        quantise(0, 1, "scalar")
+        quantise(1, 0, "scalar")
+        quantise(1, 1, "vector")
+
+        sums = {}
+        for i in range(2):
+            for h in range(2):
+                sums[i, h] = psum.tile([P, HALF], F32, name="sums%d%d" % (i, h))
+
+        def multiply(i, z, h):
+            cols = slice(h * HALF, (h + 1) * HALF)
+            nc.tensor.matmul_mx(
+                out=sums[i, h][:],
+                lhsT=codes[i, z][:].bitcast(FP8X4),
+                lhsT_scale=planes[i, z][:],
+                rhs=picked[z][:, cols].bitcast(FP8X4),
+                rhs_scale=x_planes[PLANE * z : P, cols],
+                start=(z == 0),
+                stop=(z == PASSES - 1),
+            )
+
+        for i in range(2):
+            for z in range(PASSES):
+                for h in range(2):
+                    multiply(i, z, h)
+
+        for h in range(2):
+            cols = slice(h * HALF, (h + 1) * HALF)
+            gate = keep.tile([P, HALF], F32, name="gate%d" % h)
+            nc.scalar.activation(gate[:], sums[0, h][:], SILU)
+            result = keep.tile([P, HALF], F32, name="result%d" % h)
+            nc.vector.tensor_tensor(result[:], sums[1, h][:], gate[:], MULT)
+            nc.sync.dma_start(out=out[:, cols], in_=result[:])

@@ -36,7 +36,7 @@ def tile_picked_phglu_silu_p_kernel(tc, x_words, x_scales, w1, w2, offs, out):
         nc.vector.memset(scale_table[:].bitcast(I32), 0)
         rows = x_scales.bitcast(I32).rearrange("z (r e) c -> e r z c", e=2)
         for e in range(2):
-            nc.gpsimd.dma_start(out=scale_table[e:P:PLANE, :].bitcast(I32), in_=rows[e])
+            nc.sync.dma_start(out=scale_table[e:P:PLANE, :].bitcast(I32), in_=rows[e])
 
         warm = keep.tile([P, 2], F32, name="warm")
         nc.vector.memset(warm[:, 0:1], 0.0)
@@ -45,20 +45,20 @@ def tile_picked_phglu_silu_p_kernel(tc, x_words, x_scales, w1, w2, offs, out):
         word_table = [keep.tile([P, T], U32, name="word_table%d" % z, align_bytes=64) for z in range(PASSES)]
         raw = {}
 
-        def load_words(z):
-            nc.sync.dma_start(out=word_table[z][:].bitcast(I32), in_=x_words[z].rearrange("p n t -> p (n t)").bitcast(I32))
+        def load_words(z, cols):
+            src = x_words[z].rearrange("p n t -> p (n t)").bitcast(I32)
+            nc.sync.dma_start(out=word_table[z][:, cols].bitcast(I32), in_=src[:, cols])
 
-        def load_weight(i, z):
-            raw[i, z] = keep.tile([P, PACK, N], F32, name="raw%d%d" % (i, z), align_bytes=64)
+        def load_weight(i, z, dst):
+            raw[i, z] = dst
             w = (w1, w2)[i]
-            nc.sync.dma_start(out=raw[i, z][:], in_=w[z * K_PASS : (z + 1) * K_PASS, :].rearrange("(p j) n -> p j n", j=PACK))
+            nc.sync.dma_start(out=dst, in_=w[z * K_PASS : (z + 1) * K_PASS, :].rearrange("(p j) n -> p (j n)", j=PACK))
 
-        load_words(0)
-        load_weight(0, 0)
-        load_words(1)
-        load_weight(0, 1)
-        load_weight(1, 0)
-        load_weight(1, 1)
+        early = keep.tile([P, PACK * N], F32, name="early", align_bytes=64)
+        load_words(0, slice(0, T // 4))
+        load_weight(0, 0, early[:])
+        load_words(0, slice(T // 4, T))
+        load_words(1, slice(0, T))
 
         picked_scales = keep.tile([P, S], U8, name="picked_scales", align_bytes=64)
         nc.vector.tensor_copy(picked_scales[:], scale_table[:].indirect(offsets[:]))
@@ -66,41 +66,48 @@ def tile_picked_phglu_silu_p_kernel(tc, x_words, x_scales, w1, w2, offs, out):
         nc.vector.tensor_copy(x_planes[:].bitcast(I32), picked_scales[:].bitcast(I32))
         for z in range(PASSES):
             for e in range(2):
-                nc.scalar.dma_start(
+                nc.sync.dma_start(
                     out=x_planes[PLANE * z + 2 + e : P : 32, :].bitcast(I32),
                     in_=picked_scales[16 + PLANE * z + e : P : 32, :].bitcast(I32),
                 )
 
         picked = [keep.tile([P, S], U32, name="picked%d" % z, align_bytes=64) for z in range(PASSES)]
-        nc.vector.tensor_copy(picked[0][:], word_table[0][:].indirect(offsets[:]))
 
         codes, planes = {}, {}
 
-        def quantise(i, z, engine):
-            grouped = keep.tile([P, N, PACK], BF16, name="grouped%d%d" % (i, z), align_bytes=64)
+        def quantise(i, z, on_scalar):
+            grouped = keep.tile([P, N, PACK], BF16, name="grouped%d%d" % (i, z), tag="stage%d%d" % (i, z), align_bytes=64)
             dst = grouped[:].rearrange("p (c i) j -> p c j i", i=4)
-            src = raw[i, z][:].rearrange("p j (c i) -> p c j i", i=4)
-            if engine == "scalar":
-                nc.scalar.copy(dst, src)
-            else:
-                nc.vector.tensor_copy(dst, src)
+            src = raw[i, z].rearrange("p (j c i) -> p c j i", j=PACK, i=4)
             codes[i, z] = keep.tile([P, N], U32, name="codes%d%d" % (i, z), align_bytes=64)
             planes[i, z] = keep.tile([P, N], U8, name="planes%d%d" % (i, z), align_bytes=64)
-            nc.vector.quantize_mx(
-                out=codes[i, z][:].bitcast(FP8X4),
-                scales=planes[i, z][:],
-                in_=grouped[:].rearrange("p n j -> p (n j)"),
-            )
+            if on_scalar:
+                nc.scalar.copy(dst, src)
+                parts = [slice(0, N)]
+            else:
+                parts = [slice(0, N // 2), slice(N // 2, N)]
+                for m in parts:
+                    nc.vector.tensor_copy(dst[:, m.start // 4 : m.stop // 4], src[:, m.start // 4 : m.stop // 4])
+            for m in parts:
+                nc.vector.quantize_mx(
+                    out=codes[i, z][:, m].bitcast(FP8X4),
+                    scales=planes[i, z][:, m],
+                    in_=grouped[:, m, :].rearrange("p n j -> p (n j)"),
+                )
 
-        quantise(0, 0, "scalar")
+        quantise(0, 0, True)
+        late = keep.tile([P, 3 * PACK * N], F32, name="late", tag="stage00", align_bytes=64)
+        for n, (i, z) in enumerate(((0, 1), (1, 0), (1, 1))):
+            load_weight(i, z, late[:, n * PACK * N : (n + 1) * PACK * N])
+        nc.vector.tensor_copy(picked[0][:], word_table[0][:].indirect(offsets[:]))
         for h in range(2):
             nc.vector.tensor_copy(
                 picked[1][:, h * HALF : (h + 1) * HALF],
                 word_table[1][:].indirect(offsets[:, h * HALF // 16 : (h + 1) * HALF // 16]),
             )
-        quantise(0, 1, "scalar")
-        quantise(1, 0, "scalar")
-        quantise(1, 1, "vector")
+        quantise(0, 1, True)
+        quantise(1, 0, True)
+        quantise(1, 1, False)
 
         sums = {}
         for i in range(2):

@@ -21,19 +21,22 @@ K_PASS = P * PACK
 PASSES = K // K_PASS
 HALF = S // 2
 PLANE = 8
+LEAD = T // 4
+RAW = PACK * N * 4
 
 
 def tile_picked_phglu_silu_p_kernel(tc, x_words, x_scales, w1, w2, offs, out):
     nc = tc.nc
     with ExitStack() as ctx:
         keep = ctx.enter_context(tc.tile_pool(name="keep", bufs=1))
+        held = ctx.enter_context(tc.tile_pool(name="held", bufs=1))
         psum = ctx.enter_context(tc.psum_pool(name="psum", bufs=1))
 
         offsets = keep.tile([P, S // 16], U16, name="offsets")
         nc.sync.dma_start(offsets[:], offs)
 
-        scale_table = keep.tile([P, T], U8, name="scale_table", align_bytes=64)
-        nc.vector.memset(scale_table[:].bitcast(I32), 0)
+        scale_table = held.tile([P, T], U8, name="scale_table", align_bytes=64, offset=2 * RAW)
+        nc.gpsimd.memset(scale_table[:].bitcast(I32), 0)
         rows = x_scales.bitcast(I32).rearrange("z (r e) c -> e r z c", e=2)
         for e in range(2):
             nc.sync.dma_start(out=scale_table[e:P:PLANE, :].bitcast(I32), in_=rows[e])
@@ -42,82 +45,83 @@ def tile_picked_phglu_silu_p_kernel(tc, x_words, x_scales, w1, w2, offs, out):
         nc.vector.memset(warm[:, 0:1], 0.0)
         nc.scalar.activation(warm[:, 1:2], warm[:, 0:1], SILU)
 
-        word_table = [keep.tile([P, T], U32, name="word_table%d" % z, align_bytes=64) for z in range(PASSES)]
         raw = {}
+        word_table = [keep.tile([P, T], U32, name="word_table0", align_bytes=64)]
 
         def load_words(z, cols):
             src = x_words[z].rearrange("p n t -> p (n t)").bitcast(I32)
             nc.sync.dma_start(out=word_table[z][:, cols].bitcast(I32), in_=src[:, cols])
 
         def load_weight(i, z, dst):
-            raw[i, z] = dst
+            raw[i, z] = dst[:]
             w = (w1, w2)[i]
-            nc.sync.dma_start(out=dst, in_=w[z * K_PASS : (z + 1) * K_PASS, :].rearrange("(p j) n -> p (j n)", j=PACK))
+            nc.sync.dma_start(out=dst[:], in_=w[z * K_PASS : (z + 1) * K_PASS, :].rearrange("(p j) n -> p (j n)", j=PACK))
 
-        early = keep.tile([P, PACK * N], F32, name="early", align_bytes=64)
-        load_words(0, slice(0, T // 4))
-        load_weight(0, 0, early[:])
-        load_words(0, slice(T // 4, T))
-        load_words(1, slice(0, T))
+        load_weight(0, 0, held.tile([P, PACK * N], F32, name="raw00", align_bytes=64, offset=4 * RAW))
+        load_weight(1, 0, keep.tile([P, PACK * N], F32, name="raw10", align_bytes=64))
+        load_weight(0, 1, keep.tile([P, PACK * N], F32, name="raw01", align_bytes=64))
+        load_words(0, slice(0, T))
 
-        picked_scales = keep.tile([P, S], U8, name="picked_scales", align_bytes=64)
+        picked_scales = held.tile([P, S], U8, name="picked_scales", align_bytes=64, offset=RAW - S // 2)
         nc.vector.tensor_copy(picked_scales[:], scale_table[:].indirect(offsets[:]))
+        word_table.append(held.tile([P, T], U32, name="word_table1", align_bytes=64, offset=4 * RAW))
+        load_words(1, slice(0, 5 * T // 8))
         x_planes = keep.tile([P, S], U8, name="x_planes", align_bytes=64)
         nc.vector.tensor_copy(x_planes[:].bitcast(I32), picked_scales[:].bitcast(I32))
         for z in range(PASSES):
             for e in range(2):
                 nc.sync.dma_start(
                     out=x_planes[PLANE * z + 2 + e : P : 32, :].bitcast(I32),
-                    in_=picked_scales[16 + PLANE * z + e : P : 32, :].bitcast(I32),
+                    in_=x_planes[16 + PLANE * z + e : P : 32, :].bitcast(I32),
                 )
-
+        load_words(1, slice(5 * T // 8, T))
+        load_weight(1, 1, held.tile([P, PACK * N], F32, name="raw11", align_bytes=64, offset=0 * RAW))
         picked = [keep.tile([P, S], U32, name="picked%d" % z, align_bytes=64) for z in range(PASSES)]
+        codes, planes, grouped = {}, {}, {}
 
-        codes, planes = {}, {}
-
-        def quantise(i, z, on_scalar):
-            grouped = keep.tile([P, N, PACK], BF16, name="grouped%d%d" % (i, z), tag="stage%d%d" % (i, z), align_bytes=64)
-            dst = grouped[:].rearrange("p (c i) j -> p c j i", i=4)
+        def cast(i, z, copy, m):
+            if (i, z) not in grouped:
+                grouped[i, z] = keep.tile([P, N, PACK], BF16, name="grouped%d%d" % (i, z), align_bytes=64)
+            dst = grouped[i, z][:].rearrange("p (c i) j -> p c j i", i=4)
             src = raw[i, z].rearrange("p (j c i) -> p c j i", j=PACK, i=4)
-            codes[i, z] = keep.tile([P, N], U32, name="codes%d%d" % (i, z), align_bytes=64)
-            planes[i, z] = keep.tile([P, N], U8, name="planes%d%d" % (i, z), align_bytes=64)
-            if on_scalar:
-                nc.scalar.copy(dst, src)
-                parts = [slice(0, N)]
-            else:
-                parts = [slice(0, N // 2), slice(N // 2, N)]
-                for m in parts:
-                    nc.vector.tensor_copy(dst[:, m.start // 4 : m.stop // 4], src[:, m.start // 4 : m.stop // 4])
-            for m in parts:
-                nc.vector.quantize_mx(
-                    out=codes[i, z][:, m].bitcast(FP8X4),
-                    scales=planes[i, z][:, m],
-                    in_=grouped[:, m, :].rearrange("p n j -> p (n j)"),
-                )
+            copy(dst[:, m.start // 4 : m.stop // 4], src[:, m.start // 4 : m.stop // 4])
 
-        quantise(0, 0, True)
-        late = keep.tile([P, 3 * PACK * N], F32, name="late", tag="stage00", align_bytes=64)
-        for n, (i, z) in enumerate(((0, 1), (1, 0), (1, 1))):
-            load_weight(i, z, late[:, n * PACK * N : (n + 1) * PACK * N])
-        nc.vector.tensor_copy(picked[0][:], word_table[0][:].indirect(offsets[:]))
-        for h in range(2):
-            nc.vector.tensor_copy(
-                picked[1][:, h * HALF : (h + 1) * HALF],
-                word_table[1][:].indirect(offsets[:, h * HALF // 16 : (h + 1) * HALF // 16]),
+        def quantise(i, z, m):
+            if (i, z) not in codes:
+                if (i, z) == (0, 0):
+                    codes[i, z] = held.tile([P, N], U32, name="codes00", align_bytes=64, offset=2 * RAW)
+                else:
+                    codes[i, z] = keep.tile([P, N], U32, name="codes%d%d" % (i, z), align_bytes=64)
+                planes[i, z] = keep.tile([P, N], U8, name="planes%d%d" % (i, z), align_bytes=64)
+            nc.vector.quantize_mx(
+                out=codes[i, z][:, m].bitcast(FP8X4),
+                scales=planes[i, z][:, m],
+                in_=grouped[i, z][:, m, :].rearrange("p n j -> p (n j)"),
             )
-        quantise(0, 1, True)
-        quantise(1, 0, True)
-        quantise(1, 1, False)
+
+        def gather(z, cols):
+            nc.vector.tensor_copy(picked[z][:, cols], word_table[z][:].indirect(offsets[:, cols.start // 16 : cols.stop // 16]))
+
+        cast(0, 0, nc.scalar.copy, slice(0, N))
+        quantise(0, 0, slice(0, N))
+        cast(1, 0, nc.scalar.copy, slice(0, N))
+        quantise(1, 0, slice(0, N))
+        cast(0, 1, nc.scalar.copy, slice(0, N))
+        quantise(0, 1, slice(0, N))
+        gather(0, slice(0, HALF))
+        gather(0, slice(HALF, S))
+        gather(1, slice(0, HALF))
+        gather(1, slice(HALF, S))
+        cast(1, 1, nc.scalar.copy, slice(0, N))
+        quantise(1, 1, slice(0, N))
 
         sums = {}
-        for i in range(2):
-            for h in range(2):
-                sums[i, h] = psum.tile([P, HALF], F32, name="sums%d%d" % (i, h))
 
-        def multiply(i, z, h):
-            cols = slice(h * HALF, (h + 1) * HALF)
+        def multiply(i, z, cols):
+            if (i, cols.start) not in sums:
+                sums[i, cols.start] = psum.tile([P, cols.stop - cols.start], F32, name="sums%d_%d" % (i, cols.start))
             nc.tensor.matmul_mx(
-                out=sums[i, h][:],
+                out=sums[i, cols.start][:],
                 lhsT=codes[i, z][:].bitcast(FP8X4),
                 lhsT_scale=planes[i, z][:],
                 rhs=picked[z][:, cols].bitcast(FP8X4),
@@ -126,15 +130,28 @@ def tile_picked_phglu_silu_p_kernel(tc, x_words, x_scales, w1, w2, offs, out):
                 stop=(z == PASSES - 1),
             )
 
-        for i in range(2):
-            for z in range(PASSES):
-                for h in range(2):
-                    multiply(i, z, h)
-
-        for h in range(2):
-            cols = slice(h * HALF, (h + 1) * HALF)
-            gate = keep.tile([P, HALF], F32, name="gate%d" % h)
-            nc.scalar.activation(gate[:], sums[0, h][:], SILU)
-            result = keep.tile([P, HALF], F32, name="result%d" % h)
-            nc.vector.tensor_tensor(result[:], sums[1, h][:], gate[:], MULT)
-            nc.sync.dma_start(out=out[:, cols], in_=result[:])
+        gate = held.tile([P, S], F32, name="gate", align_bytes=64, offset=0)
+        result = keep.tile([P, S], F32, name="result")
+        multiply(0, 0, slice(0, 256))
+        multiply(1, 0, slice(0, 128))
+        multiply(1, 0, slice(128, 256))
+        multiply(0, 0, slice(256, 384))
+        multiply(0, 0, slice(384, 512))
+        multiply(1, 0, slice(256, 384))
+        multiply(1, 0, slice(384, 512))
+        multiply(0, 1, slice(0, 256))
+        multiply(0, 1, slice(256, 384))
+        multiply(0, 1, slice(384, 512))
+        multiply(1, 1, slice(0, 128))
+        multiply(1, 1, slice(128, 256))
+        multiply(1, 1, slice(256, 384))
+        multiply(1, 1, slice(384, 512))
+        nc.scalar.activation(gate[:, 0:256], sums[0, 0][:], SILU)
+        nc.scalar.activation(gate[:, 256:384], sums[0, 256][:], SILU)
+        nc.scalar.activation(gate[:, 384:512], sums[0, 384][:], SILU)
+        nc.vector.tensor_tensor(result[:, 0:128], sums[1, 0][:], gate[:, 0:128], MULT)
+        nc.vector.tensor_tensor(result[:, 128:256], sums[1, 128][:], gate[:, 128:256], MULT)
+        nc.sync.dma_start(out=out[:, 0:256], in_=result[:, 0:256])
+        nc.vector.tensor_tensor(result[:, 256:384], sums[1, 256][:], gate[:, 256:384], MULT)
+        nc.vector.tensor_tensor(result[:, 384:512], sums[1, 384][:], gate[:, 384:512], MULT)
+        nc.sync.dma_start(out=out[:, 256:512], in_=result[:, 256:512])

@@ -14,6 +14,7 @@ U8 = mybir.dt.uint8
 FP8X4 = mybir.dt.float8_e4m3fn_x4
 SILU = mybir.ActivationFunctionType.Silu
 MULT = mybir.AluOpType.mult
+ADD = mybir.AluOpType.add
 
 P = 128
 PACK = 4
@@ -112,7 +113,15 @@ def tile_picked_phglu_silu_p_kernel(tc, x_words, x_scales, w1, w2, offs, out):
         gather(0, slice(HALF, S))
         gather(1, slice(0, HALF))
         gather(1, slice(HALF, S))
-        cast(1, 1, nc.scalar.copy, slice(0, N))
+        cast(1, 1, nc.scalar.copy, slice(0, N // 2))
+        nc.gpsimd.tensor_scalar(
+            grouped[1, 1][:, N // 2 : N, :],
+            raw[1, 1].rearrange("p (j n) -> p n j", j=PACK)[:, N // 2 : N, :],
+            1.0,
+            0.0,
+            MULT,
+            ADD,
+        )
         quantise(1, 1, slice(0, N))
 
         sums = {}

@@ -34,13 +34,9 @@ def tile_picked_phglu_silu_p_kernel(tc, x_words, x_scales, w1, w2, offs, out):
         psum = ctx.enter_context(tc.psum_pool(name="psum", bufs=1))
 
         offsets = keep.tile([P, S // 16], U16, name="offsets")
-        nc.sync.dma_start(offsets[:], offs)
 
         scale_table = held.tile([P, T], U8, name="scale_table", align_bytes=64, offset=2 * RAW)
-        nc.gpsimd.memset(scale_table[:].bitcast(I32), 0)
-        rows = x_scales.bitcast(I32).rearrange("z (r e) c -> e r z c", e=2)
-        for e in range(2):
-            nc.sync.dma_start(out=scale_table[e:P:PLANE, :].bitcast(I32), in_=rows[e])
+        nc.vector.memset(scale_table[:].bitcast(I32), 0)
 
         warm = keep.tile([P, 2], F32, name="warm")
         nc.vector.memset(warm[:, 0:1], 0.0)
@@ -59,6 +55,10 @@ def tile_picked_phglu_silu_p_kernel(tc, x_words, x_scales, w1, w2, offs, out):
             nc.sync.dma_start(out=dst[:], in_=w[z * K_PASS : (z + 1) * K_PASS, :].rearrange("(p j) n -> p (j n)", j=PACK))
 
         load_weight(0, 0, held.tile([P, PACK * N], F32, name="raw00", align_bytes=64, offset=4 * RAW))
+        nc.sync.dma_start(offsets[:], offs)
+        rows = x_scales.bitcast(I32).rearrange("z (r e) c -> e r z c", e=2)
+        for e in range(2):
+            nc.sync.dma_start(out=scale_table[e:P:PLANE, :].bitcast(I32), in_=rows[e])
         load_weight(1, 0, keep.tile([P, PACK * N], F32, name="raw10", align_bytes=64))
         load_weight(0, 1, keep.tile([P, PACK * N], F32, name="raw01", align_bytes=64))
         load_words(0, slice(0, T))

@@ -14,7 +14,6 @@ U8 = mybir.dt.uint8
 FP8X4 = mybir.dt.float8_e4m3fn_x4
 SILU = mybir.ActivationFunctionType.Silu
 MULT = mybir.AluOpType.mult
-ADD = mybir.AluOpType.add
 
 P = 128
 PACK = 4
@@ -83,9 +82,9 @@ def tile_picked_phglu_silu_p_kernel(tc, x_words, x_scales, w1, w2, offs, out):
         def cast(i, z, copy, m):
             if (i, z) not in grouped:
                 grouped[i, z] = keep.tile([P, N, PACK], BF16, name="grouped%d%d" % (i, z), align_bytes=64)
-            dst = grouped[i, z][:].rearrange("p (c i) j -> p c j i", i=4)
-            src = raw[i, z].rearrange("p (j c i) -> p c j i", j=PACK, i=4)
-            copy(dst[:, m.start // 4 : m.stop // 4], src[:, m.start // 4 : m.stop // 4])
+            dst = grouped[i, z][:].rearrange("p (c i) j -> p c j i", i=2)
+            src = raw[i, z].rearrange("p (j c i) -> p c j i", j=PACK, i=2)
+            copy(dst[:, m.start // 2 : m.stop // 2], src[:, m.start // 2 : m.stop // 2])
 
         def quantise(i, z, m):
             if (i, z) not in codes:
@@ -113,15 +112,7 @@ def tile_picked_phglu_silu_p_kernel(tc, x_words, x_scales, w1, w2, offs, out):
         gather(0, slice(HALF, S))
         gather(1, slice(0, HALF))
         gather(1, slice(HALF, S))
-        cast(1, 1, nc.scalar.copy, slice(0, N // 2))
-        nc.gpsimd.tensor_scalar(
-            grouped[1, 1][:, N // 2 : N, :],
-            raw[1, 1].rearrange("p (j n) -> p n j", j=PACK)[:, N // 2 : N, :],
-            1.0,
-            0.0,
-            MULT,
-            ADD,
-        )
+        cast(1, 1, nc.scalar.copy, slice(0, N))
         quantise(1, 1, slice(0, N))
 
         sums = {}

@@ -102,11 +102,14 @@ def tile_picked_phglu_silu_p_kernel(tc, x_words, x_scales, w1, w2, offs, out):
         def gather(z, cols):
             nc.vector.tensor_copy(picked[z][:, cols], word_table[z][:].indirect(offsets[:, cols.start // 16 : cols.stop // 16]))
 
-        cast(0, 0, nc.scalar.copy, slice(0, N))
+        cast(0, 0, nc.scalar.copy, slice(0, N // 2))
+        cast(0, 0, nc.scalar.copy, slice(N // 2, N))
         quantise(0, 0, slice(0, N))
-        cast(1, 0, nc.scalar.copy, slice(0, N))
+        cast(1, 0, nc.scalar.copy, slice(0, N // 2))
+        cast(1, 0, nc.scalar.copy, slice(N // 2, N))
         quantise(1, 0, slice(0, N))
-        cast(0, 1, nc.scalar.copy, slice(0, N))
+        cast(0, 1, nc.scalar.copy, slice(0, N // 2))
+        cast(0, 1, nc.scalar.copy, slice(N // 2, N))
         quantise(0, 1, slice(0, N))
         gather(0, slice(0, HALF))
         gather(0, slice(HALF, S))

@@ -59,8 +59,8 @@ def tile_picked_phglu_silu_p_kernel(tc, x_words, x_scales, w1, w2, offs, out):
         for e in range(2):
             nc.sync.dma_start(out=scale_table[e:P:PLANE, :].bitcast(I32), in_=rows[e])
         load_weight(1, 0, keep.tile([P, PACK * N], F32, name="raw10", align_bytes=64))
-        load_weight(0, 1, keep.tile([P, PACK * N], F32, name="raw01", align_bytes=64))
         load_words(0, slice(0, T))
+        load_weight(0, 1, keep.tile([P, PACK * N], F32, name="raw01", align_bytes=64))
 
         picked_scales = held.tile([P, S], U8, name="picked_scales", align_bytes=64, offset=RAW - S // 2)
         nc.vector.tensor_copy(picked_scales[:], scale_table[:].indirect(offsets[:]))
@@ -108,11 +108,11 @@ def tile_picked_phglu_silu_p_kernel(tc, x_words, x_scales, w1, w2, offs, out):
         cast(1, 0, nc.scalar.copy, slice(0, N // 2))
         cast(1, 0, nc.scalar.copy, slice(N // 2, N))
         quantise(1, 0, slice(0, N))
+        gather(0, slice(0, HALF))
+        gather(0, slice(HALF, S))
         cast(0, 1, nc.scalar.copy, slice(0, N // 2))
         cast(0, 1, nc.scalar.copy, slice(N // 2, N))
         quantise(0, 1, slice(0, N))
-        gather(0, slice(0, HALF))
-        gather(0, slice(HALF, S))
         gather(1, slice(0, HALF))
         gather(1, slice(HALF, S))
         cast(1, 1, nc.scalar.copy, slice(0, N))

@@ -14,6 +14,7 @@ U8 = mybir.dt.uint8
 FP8X4 = mybir.dt.float8_e4m3fn_x4
 SILU = mybir.ActivationFunctionType.Silu
 MULT = mybir.AluOpType.mult
+ADD = mybir.AluOpType.add
 
 P = 128
 PACK = 4
@@ -21,6 +22,7 @@ K_PASS = P * PACK
 PASSES = K // K_PASS
 HALF = S // 2
 PLANE = 8
+SCALAR_SHARE = 80
 LEAD = T // 4
 RAW = PACK * N * 4
 
@@ -86,6 +88,10 @@ def tile_picked_phglu_silu_p_kernel(tc, x_words, x_scales, w1, w2, offs, out):
             src = raw[i, z].rearrange("p (j c i) -> p c j i", j=PACK, i=2)
             copy(dst[:, m.start // 2 : m.stop // 2], src[:, m.start // 2 : m.stop // 2])
 
+        def cast_gpsimd(i, z, m):
+            src = raw[i, z].rearrange("p (j n) -> p n j", j=PACK)
+            nc.gpsimd.tensor_scalar(grouped[i, z][:, m, :], src[:, m, :], 1.0, 0.0, MULT, ADD)
+
         def quantise(i, z, m):
             if (i, z) not in codes:
                 if (i, z) == (0, 0):
@@ -115,7 +121,8 @@ def tile_picked_phglu_silu_p_kernel(tc, x_words, x_scales, w1, w2, offs, out):
         quantise(0, 1, slice(0, N))
         gather(1, slice(0, HALF))
         gather(1, slice(HALF, S))
-        cast(1, 1, nc.scalar.copy, slice(0, N))
+        cast(1, 1, nc.scalar.copy, slice(0, SCALAR_SHARE))
+        cast_gpsimd(1, 1, slice(SCALAR_SHARE, N))
         quantise(1, 1, slice(0, N))
 
         sums = {}

@@ -23,7 +23,6 @@ PASSES = K // K_PASS
 HALF = S // 2
 PLANE = 8
 SCALAR_SHARE = 80
-LEAD = T // 4
 RAW = PACK * N * 4
 
 
@@ -55,14 +54,16 @@ def tile_picked_phglu_silu_p_kernel(tc, x_words, x_scales, w1, w2, offs, out):
             w = (w1, w2)[i]
             nc.sync.dma_start(out=dst[:], in_=w[z * K_PASS : (z + 1) * K_PASS, :].rearrange("(p j) n -> p (j n)", j=PACK))
 
-        load_weight(0, 0, held.tile([P, PACK * N], F32, name="raw00", align_bytes=64, offset=4 * RAW))
+        load_weight(1, 0, held.tile([P, PACK * N], F32, name="raw10", align_bytes=64, offset=4 * RAW))
         nc.sync.dma_start(offsets[:], offs)
         rows = x_scales.bitcast(I32).rearrange("z (r e) c -> e r z c", e=2)
         for e in range(2):
             nc.sync.dma_start(out=scale_table[e:P:PLANE, :].bitcast(I32), in_=rows[e])
-        load_weight(1, 0, keep.tile([P, PACK * N], F32, name="raw10", align_bytes=64))
+        raw_w1 = keep.tile([P, PASSES, PACK * N], F32, name="raw_w1", align_bytes=64)
+        nc.sync.dma_start(out=raw_w1[:], in_=w1.rearrange("(z p j) n -> p z (j n)", z=PASSES, j=PACK))
+        for z in range(PASSES):
+            raw[0, z] = raw_w1[:, z, :]
         load_words(0, slice(0, T))
-        load_weight(0, 1, keep.tile([P, PACK * N], F32, name="raw01", align_bytes=64))
 
         picked_scales = held.tile([P, S], U8, name="picked_scales", align_bytes=64, offset=RAW - S // 2)
         nc.vector.tensor_copy(picked_scales[:], scale_table[:].indirect(offsets[:]))
@@ -94,8 +95,8 @@ def tile_picked_phglu_silu_p_kernel(tc, x_words, x_scales, w1, w2, offs, out):
 
         def quantise(i, z, m):
             if (i, z) not in codes:
-                if (i, z) == (0, 0):
-                    codes[i, z] = held.tile([P, N], U32, name="codes00", align_bytes=64, offset=2 * RAW)
+                if (i, z) == (1, 0):
+                    codes[i, z] = held.tile([P, N], U32, name="codes10", align_bytes=64, offset=2 * RAW)
                 else:
                     codes[i, z] = keep.tile([P, N], U32, name="codes%d%d" % (i, z), align_bytes=64)
                 planes[i, z] = keep.tile([P, N], U8, name="planes%d%d" % (i, z), align_bytes=64)
@@ -108,17 +109,12 @@ def tile_picked_phglu_silu_p_kernel(tc, x_words, x_scales, w1, w2, offs, out):
         def gather(z, cols):
             nc.vector.tensor_copy(picked[z][:, cols], word_table[z][:].indirect(offsets[:, cols.start // 16 : cols.stop // 16]))
 
-        cast(0, 0, nc.scalar.copy, slice(0, N // 2))
-        cast(0, 0, nc.scalar.copy, slice(N // 2, N))
-        quantise(0, 0, slice(0, N))
-        cast(1, 0, nc.scalar.copy, slice(0, N // 2))
-        cast(1, 0, nc.scalar.copy, slice(N // 2, N))
-        quantise(1, 0, slice(0, N))
+        for i, z in ((1, 0), (0, 0), (0, 1)):
+            cast(i, z, nc.scalar.copy, slice(0, N // 2))
+            cast(i, z, nc.scalar.copy, slice(N // 2, N))
+            quantise(i, z, slice(0, N))
         gather(0, slice(0, HALF))
         gather(0, slice(HALF, S))
-        cast(0, 1, nc.scalar.copy, slice(0, N // 2))
-        cast(0, 1, nc.scalar.copy, slice(N // 2, N))
-        quantise(0, 1, slice(0, N))
         gather(1, slice(0, HALF))
         gather(1, slice(HALF, S))
         cast(1, 1, nc.scalar.copy, slice(0, SCALAR_SHARE))
@@ -160,8 +156,9 @@ def tile_picked_phglu_silu_p_kernel(tc, x_words, x_scales, w1, w2, offs, out):
         nc.scalar.activation(gate[:, 256:384], sums[0, 256][:], SILU)
         nc.scalar.activation(gate[:, 384:512], sums[0, 384][:], SILU)
         nc.vector.tensor_tensor(result[:, 0:128], sums[1, 0][:], gate[:, 0:128], MULT)
+        nc.sync.dma_start(out=out[:, 0:128], in_=result[:, 0:128])
         nc.vector.tensor_tensor(result[:, 128:256], sums[1, 128][:], gate[:, 128:256], MULT)
-        nc.sync.dma_start(out=out[:, 0:256], in_=result[:, 0:256])
+        nc.sync.dma_start(out=out[:, 128:256], in_=result[:, 128:256])
         nc.vector.tensor_tensor(result[:, 256:384], sums[1, 256][:], gate[:, 256:384], MULT)
         nc.vector.tensor_tensor(result[:, 384:512], sums[1, 384][:], gate[:, 384:512], MULT)
         nc.sync.dma_start(out=out[:, 256:512], in_=result[:, 256:512])

from contextlib import ExitStack

import concourse.mybir as mybir

K, T, S, N = 1024, 2048, 512, 128
FLOPS = 2 * 2 * K * S * N

F32 = mybir.dt.float32
BF16 = mybir.dt.bfloat16
I32 = mybir.dt.int32
U32 = mybir.dt.uint32
U16 = mybir.dt.uint16
U8 = mybir.dt.uint8
FP8X4 = mybir.dt.float8_e4m3fn_x4
SILU = mybir.ActivationFunctionType.Silu
MULT = mybir.AluOpType.mult
ADD = mybir.AluOpType.add

P = 128
PACK = 4
K_PASS = P * PACK
PASSES = K // K_PASS
HALF = S // 2
PLANE = 8
SCALAR_SHARE = 80
RAW = PACK * N * 4


def tile_picked_phglu_silu_p_kernel(tc, x_words, x_scales, w1, w2, offs, out):
    nc = tc.nc
    with ExitStack() as ctx:
        keep = ctx.enter_context(tc.tile_pool(name="keep", bufs=1))
        held = ctx.enter_context(tc.tile_pool(name="held", bufs=1))
        psum = ctx.enter_context(tc.psum_pool(name="psum", bufs=1))

        offsets = keep.tile([P, S // 16], U16, name="offsets")

        scale_table = held.tile([P, T], U8, name="scale_table", align_bytes=64, offset=2 * RAW)
        nc.vector.memset(scale_table[:].bitcast(I32), 0)

        warm = keep.tile([P, 2], F32, name="warm")
        nc.vector.memset(warm[:, 0:1], 0.0)
        nc.scalar.activation(warm[:, 1:2], warm[:, 0:1], SILU)

        raw = {}
        word_table = [keep.tile([P, T], U32, name="word_table0", align_bytes=64)]

        def load_words(z, cols):
            src = x_words[z].rearrange("p n t -> p (n t)").bitcast(I32)
            nc.sync.dma_start(out=word_table[z][:, cols].bitcast(I32), in_=src[:, cols])

        def load_weight(i, z, dst):
            raw[i, z] = dst[:]
            w = (w1, w2)[i]
            nc.sync.dma_start(out=dst[:], in_=w[z * K_PASS : (z + 1) * K_PASS, :].rearrange("(p j) n -> p (j n)", j=PACK))

        load_weight(1, 0, held.tile([P, PACK * N], F32, name="raw10", align_bytes=64, offset=4 * RAW))
        nc.sync.dma_start(offsets[:], offs)
        rows = x_scales.bitcast(I32).rearrange("z (r e) c -> e r z c", e=2)
        for e in range(2):
            nc.sync.dma_start(out=scale_table[e:P:PLANE, :].bitcast(I32), in_=rows[e])
        raw_w1 = keep.tile([P, PASSES, PACK * N], F32, name="raw_w1", align_bytes=64)
        nc.sync.dma_start(out=raw_w1[:], in_=w1.rearrange("(z p j) n -> p z (j n)", z=PASSES, j=PACK))
        for z in range(PASSES):
            raw[0, z] = raw_w1[:, z, :]
        load_words(0, slice(0, T))

        picked_scales = held.tile([P, S], U8, name="picked_scales", align_bytes=64, offset=RAW - S // 2)
        nc.vector.tensor_copy(picked_scales[:], scale_table[:].indirect(offsets[:]))
        word_table.append(held.tile([P, T], U32, name="word_table1", align_bytes=64, offset=4 * RAW))
        load_words(1, slice(0, 5 * T // 8))
        x_planes = keep.tile([P, S], U8, name="x_planes", align_bytes=64)
        nc.vector.tensor_copy(x_planes[:].bitcast(I32), picked_scales[:].bitcast(I32))
        for z in range(PASSES):
            for e in range(2):
                nc.sync.dma_start(
                    out=x_planes[PLANE * z + 2 + e : P : 32, :].bitcast(I32),
                    in_=x_planes[16 + PLANE * z + e : P : 32, :].bitcast(I32),
                )
        load_words(1, slice(5 * T // 8, T))
        load_weight(1, 1, held.tile([P, PACK * N], F32, name="raw11", align_bytes=64, offset=0 * RAW))
        picked = [keep.tile([P, S], U32, name="picked%d" % z, align_bytes=64) for z in range(PASSES)]
        codes, planes, grouped = {}, {}, {}

        def cast(i, z, copy, m):
            if (i, z) not in grouped:
                grouped[i, z] = keep.tile([P, N, PACK], BF16, name="grouped%d%d" % (i, z), align_bytes=64)
            dst = grouped[i, z][:].rearrange("p (c i) j -> p c j i", i=2)
            src = raw[i, z].rearrange("p (j c i) -> p c j i", j=PACK, i=2)
            copy(dst[:, m.start // 2 : m.stop // 2], src[:, m.start // 2 : m.stop // 2])

        def cast_gpsimd(i, z, m):
            src = raw[i, z].rearrange("p (j n) -> p n j", j=PACK)
            nc.gpsimd.tensor_scalar(grouped[i, z][:, m, :], src[:, m, :], 1.0, 0.0, MULT, ADD)

        def quantise(i, z, m):
            if (i, z) not in codes:
                if (i, z) == (1, 0):
                    codes[i, z] = held.tile([P, N], U32, name="codes10", align_bytes=64, offset=2 * RAW)
                else:
                    codes[i, z] = keep.tile([P, N], U32, name="codes%d%d" % (i, z), align_bytes=64)
                planes[i, z] = keep.tile([P, N], U8, name="planes%d%d" % (i, z), align_bytes=64)
            nc.vector.quantize_mx(
                out=codes[i, z][:, m].bitcast(FP8X4),
                scales=planes[i, z][:, m],
                in_=grouped[i, z][:, m, :].rearrange("p n j -> p (n j)"),
            )

        def gather(z, cols):
            nc.vector.tensor_copy(picked[z][:, cols], word_table[z][:].indirect(offsets[:, cols.start // 16 : cols.stop // 16]))

        for i, z in ((1, 0), (0, 0), (0, 1)):
            cast(i, z, nc.scalar.copy, slice(0, N // 2))
            cast(i, z, nc.scalar.copy, slice(N // 2, N))
            quantise(i, z, slice(0, N))
        gather(0, slice(0, HALF))
        gather(0, slice(HALF, S))
        gather(1, slice(0, HALF))
        gather(1, slice(HALF, S))
        cast(1, 1, nc.scalar.copy, slice(0, SCALAR_SHARE))
        cast_gpsimd(1, 1, slice(SCALAR_SHARE, N))
        quantise(1, 1, slice(0, N))

        sums = {}

        def multiply(i, z, cols):
            if (i, cols.start) not in sums:
                sums[i, cols.start] = psum.tile([P, cols.stop - cols.start], F32, name="sums%d_%d" % (i, cols.start))
            nc.tensor.matmul_mx(
                out=sums[i, cols.start][:],
                lhsT=codes[i, z][:].bitcast(FP8X4),
                lhsT_scale=planes[i, z][:],
                rhs=picked[z][:, cols].bitcast(FP8X4),
                rhs_scale=x_planes[PLANE * z : P, cols],
                start=(z == 0),
                stop=(z == PASSES - 1),
            )

        gate = held.tile([P, S], F32, name="gate", align_bytes=64, offset=0)
        result = keep.tile([P, S], F32, name="result")
        multiply(0, 0, slice(0, 256))
        multiply(1, 0, slice(0, 128))
        multiply(1, 0, slice(128, 256))
        multiply(0, 0, slice(256, 384))
        multiply(0, 0, slice(384, 512))
        multiply(1, 0, slice(256, 384))
        multiply(1, 0, slice(384, 512))
        multiply(0, 1, slice(0, 256))
        multiply(0, 1, slice(256, 384))
        multiply(0, 1, slice(384, 512))
        multiply(1, 1, slice(0, 128))
        multiply(1, 1, slice(128, 256))
        multiply(1, 1, slice(256, 384))
        multiply(1, 1, slice(384, 512))
        nc.scalar.activation(gate[:, 0:256], sums[0, 0][:], SILU)
        nc.scalar.activation(gate[:, 256:384], sums[0, 256][:], SILU)
        nc.scalar.activation(gate[:, 384:512], sums[0, 384][:], SILU)
        nc.vector.tensor_tensor(result[:, 0:128], sums[1, 0][:], gate[:, 0:128], MULT)
        nc.sync.dma_start(out=out[:, 0:128], in_=result[:, 0:128])
        nc.vector.tensor_tensor(result[:, 128:256], sums[1, 128][:], gate[:, 128:256], MULT)
        nc.sync.dma_start(out=out[:, 128:256], in_=result[:, 128:256])
        nc.vector.tensor_tensor(result[:, 256:384], sums[1, 256][:], gate[:, 256:384], MULT)
        nc.vector.tensor_tensor(result[:, 384:512], sums[1, 384][:], gate[:, 384:512], MULT)
        nc.sync.dma_start(out=out[:, 256:512], in_=result[:, 256:512])
